import numpy as np, ml_dtypes
CORES = [36,38,116,118,124,126,164,166,244,246,252,254]
N = 12
import mx_ref
NC, G = 256, 4
C = np.float32(0.0301)
BF = ml_dtypes.bfloat16
def cut(t, i, w=512):
    return t[:, w * i:w * i + w]
def tile(rs):
    return np.stack(rs, axis=2).reshape(128, -1).astype(BF)
def layer(w, X):
    out = []
    for i in range(G):
        for t in range(len(X)):
            p = mx_ref.matmul(mx_ref.quantize(cut(w, len(X) * i + t)), X[t])
            z = p if t == 0 else z + p
        out.append(z)
    return out
def act(Z):
    return [np.maximum(z, 0) * C for z in Z]
def setup_inputs(rng):
    def f(*shape):
        return mx_ref.flush((rng.standard_normal(shape, dtype=np.float32) * np.exp2(rng.integers(-2, 3, shape[:-1] + (1,)))).astype(BF))
    return {"s": f(N, 128, 4 * NC), "x": f(N, 128, 4 * NC), "w": f(N, 128, 2 * G * 512), "v": f(N, 128, 512)}
def setup_inputs_blocks(rng):
    d = setup_inputs(rng)
    for k in ("s", "x", "v"): d[k] = mx_ref.spread(d[k], rng, 4)
    for k in ("w",): d[k] = mx_ref.spread(d[k], rng, 1)
    return d
def setup_inputs_wide(rng):
    d = setup_inputs(rng)
    for k in ("s", "x", "v"): d[k] = mx_ref.flush((d[k].astype(np.float32) * np.exp2(rng.integers(-6, 7, (N, 1, 1))).astype(np.float32)).astype(BF))
    return d
def setup_inputs_zeros(rng):
    d = setup_inputs(rng); v = d["x"].reshape(N, 128, -1, 4).copy()
    v[np.broadcast_to((rng.random((N, 1, v.shape[2], 1)) < 0.33), v.shape)] = 0
    d["x"] = v.reshape(d["x"].shape)
    return d
def reference(s, x, w, v):
    q = mx_ref.quantize(s[0])
    y = np.zeros((N, 128, NC), np.float32)
    for r in range(N):
        q = mx_ref.quantize(tile(act(layer(w[r], [q, mx_ref.quantize(x[r])]))))
        y[r] = mx_ref.matmul(mx_ref.quantize(v[r]), q)
    return {"y": y}

@@ -1,0 +1,252 @@
+import numpy as np
+from concourse.mybir import dt, AluOpType, ActivationFunctionType
+
+HALF = 128
+EL = 4 * HALF
+G = 4
+WCH = 2
+WW = 2 * G * HALF // WCH
+SCALE = float(np.float32(0.0301))
+BANK = 512
+
+SCRATCH = {
+    "wb": ("sbuf", [128, 2 * G * EL], "bfloat16"),
+    "xb": ("sbuf", [128, 4 * EL], "bfloat16"),
+    "vb": ("sbuf", [128, EL], "bfloat16"),
+    "wc": ("sbuf", [128, 2 * G * HALF], "float8_e4m3fn_x4"), "wp": ("sbuf", [128, 2 * G * HALF], "uint8"),
+    "pc": ("sbuf", [128, 2 * G * HALF], "float8_e4m3fn_x4"), "pp": ("sbuf", [128, 2 * G * HALF], "uint8"),
+    "xc": ("sbuf", [128, 4 * HALF], "float8_e4m3fn_x4"), "xp": ("sbuf", [128, 4 * HALF], "uint8"),
+    "ic": ("sbuf", [128, 2 * HALF], "float8_e4m3fn_x4"), "ip": ("sbuf", [128, 2 * HALF], "uint8"),
+    "vc": ("sbuf", [128, HALF], "float8_e4m3fn_x4"), "vp": ("sbuf", [128, HALF], "uint8"),
+    "qi": ("sbuf", [128, HALF], "float8_e4m3fn_x4"), "qip": ("sbuf", [128, HALF], "uint8"),
+    "qm": ("sbuf", [128, HALF], "float8_e4m3fn_x4"), "qmp": ("sbuf", [128, HALF], "uint8"),
+    "qo": ("sbuf", [128, HALF], "float8_e4m3fn_x4"), "qop": ("sbuf", [128, HALF], "uint8"),
+    "qf": ("sbuf", [128, HALF], "float8_e4m3fn_x4"), "qfp": ("sbuf", [128, HALF], "uint8"),
+    "h0": ("sbuf", [128, EL], "bfloat16"), "h1": ("sbuf", [128, EL], "bfloat16"),
+    "ys": ("sbuf", [128, 2 * HALF], "float32"),
+    "z": ("psum", [128, 2 * G * BANK], "float32"),
+}
+SEMAPHORES = (["l_xp", "l_xo", "l_v", "k_xp", "k_xo", "k_v", "e_x", "arr", "feed", "a0", "a1", "k_m", "k_o",
+               "my0", "my1", "cy0", "cy1", "sy", "sent"]
+              + ["l_w%d" % c for c in range(WCH)] + ["k_w%d" % c for c in range(WCH)] + ["e_w%d" % c for c in range(WCH)]
+              + ["m%d_%d" % (j, i) for j in range(2) for i in range(G)])
+
+_CACHE = {}
+
+
+def _plan(cores, topo):
+    if "p" in _CACHE:
+        return _CACHE["p"]
+    chips = len(cores) // 2
+    for k in range(chips):
+        a, b = cores[2 * k], cores[2 * k + 1]
+        if (topo.host(a), topo.chip(a)) != (topo.host(b), topo.chip(b)):
+            raise ValueError("ranks 2k and 2k+1 must share a chip")
+    hop, step = 3.0, 1.0
+    best = None
+    for code in range(2 ** chips):
+        lo = [(code >> k) & 1 for k in range(chips)]
+        t, done, ok, clash = [0.0, 0.0], [0.0, 0.0], True, 0
+        passed, first = [False] * chips, [False] * chips
+        for k in range(chips):
+            for h in (0, 1):
+                done[h] = t[h] + 2 * step if k else (step if lo[0] == h else 2 * step)
+            if k == chips - 1:
+                break
+            for h in (0, 1):
+                src = cores[2 * k + (0 if lo[k] == h else 1)]
+                dst = cores[2 * k + 2 + (0 if lo[k + 1] == h else 1)]
+                if topo.may_write(src, dst):
+                    t[h] = done[h] + hop
+                elif lo[k] == h and topo.may_write(cores[2 * k + 1], dst):
+                    t[h] = done[h] + 2 * hop
+                    passed[k] = True
+                    first[k] = done[h] + hop < done[1 - h]
+                    clash += abs(done[h] + hop - done[1 - h]) < 2 * step
+                else:
+                    ok = False
+        if not ok:
+            continue
+        end = [t[h] + 2 * step + hop if lo[-1] == h else t[h] + step + hop for h in (0, 1)]
+        key = (max(end), clash, sum(end), code)
+        if best is None or key < best[0]:
+            best = (key, lo, passed, first)
+    _CACHE["p"] = best[1:]
+    return _CACHE["p"]
+
+
+def rank_program(g, core, T, topo):
+    rank = T.rank_of(core)
+    if rank is None:
+        return
+    cores = [int(c) for c in T.cores]
+    lo, passed, first = _plan(cores, topo)
+    k, pos, last = rank // 2, rank % 2, len(cores) // 2 - 1
+    partner = cores[2 * k + 1 - pos]
+    mine = lo[k] if pos == 0 else 1 - lo[k]
+    other = 1 - mine
+    S, te, ve, se, sy = T.sem, g.tensor, g.vector, g.scalar, g.sync
+    head = rank == 0
+    sent = [0]
+
+    def engines(src, dst):
+        return bin(topo.mask(src, dst)).count("1")
+
+    def owner(chip, h):
+        return cores[2 * chip + (0 if lo[chip] == h else 1)]
+
+    def send(dst, dc, dp, sc, sp, sem):
+        rid, pid = topo.addr(dst, core)
+        mask = topo.mask(core, dst)
+        g.remote_dma(dc.bitcast(dt.uint8), sc.bitcast(dt.uint8), sem, S.sent, pid, rid, mask)
+        g.remote_dma(dp, sp, sem, S.sent, pid, rid, mask)
+        sent[0] += 2 * engines(core, dst)
+
+    sy.dma_start(T.xb[:, EL:2 * EL], T.x[:, EL * other:EL * other + EL]).then_inc(S.l_xp, 16)
+    if head:
+        sy.dma_start(T.xb[:, 2 * EL:3 * EL], T.s[:, EL * other:EL * other + EL]).then_inc(S.l_xp, 16)
+    for c in range(WCH):
+        (se if c % 2 == 0 else sy).dma_start(T.wb[:, 4 * WW * c:4 * WW * (c + 1)],
+                                             T.w[:, 4 * WW * c:4 * WW * (c + 1)]).then_inc(S["l_w%d" % c], 16)
+    se.dma_start(T.xb[:, 0:EL], T.x[:, EL * mine:EL * mine + EL]).then_inc(S.l_xo, 16)
+    if head:
+        se.dma_start(T.xb[:, 3 * EL:4 * EL], T.s[:, EL * mine:EL * mine + EL]).then_inc(S.l_xo, 16)
+    sy.wait_ge(S["k_w%d" % (WCH - 1)], 1)
+    sy.dma_start(T.vb[:], T.v[:]).then_inc(S.l_v, 16)
+
+    npar = 2 * HALF if head else HALF
+    ve.wait_ge(S.l_xp, 32 if head else 16)
+    ve.quantize_mx(T.xc[:, HALF:HALF + npar], T.xp[:, HALF:HALF + npar], T.xb[:, EL:EL + 4 * npar]).then_inc(S.k_xp, 1)
+    for c in range(WCH):
+        ve.wait_ge(S["l_w%d" % c], 16)
+        ve.quantize_mx(T.wc[:, WW * c:WW * (c + 1)], T.wp[:, WW * c:WW * (c + 1)],
+                       T.wb[:, 4 * WW * c:4 * WW * (c + 1)]).then_inc(S["k_w%d" % c], 1)
+    ve.wait_ge(S.l_xo, 32 if head else 16)
+    ve.quantize_mx(T.xc[:, 0:HALF], T.xp[:, 0:HALF], T.xb[:, 0:EL]).then_inc(S.k_xo, 1)
+    if head:
+        ve.quantize_mx(T.xc[:, 3 * HALF:4 * HALF], T.xp[:, 3 * HALF:4 * HALF], T.xb[:, 3 * EL:4 * EL]).then_inc(S.k_xo, 1)
+    n_xo = 2 if head else 1
+
+    def quantise_v():
+        ve.wait_ge(S.l_v, 16)
+        ve.quantize_mx(T.vc[:], T.vp[:], T.vb[:]).then_inc(S.k_v, 1)
+
+    if k:
+        quantise_v()
+
+    g.wait_ge(S.k_xp, 1)
+    send(partner, T.ic[:, 0:npar], T.ip[:, 0:npar], T.xc[:, HALF:HALF + npar], T.xp[:, HALF:HALF + npar], S.e_x)
+    for c in range(WCH):
+        g.wait_ge(S["k_w%d" % c], 1)
+        send(partner, T.pc[:, WW * c:WW * (c + 1)], T.pp[:, WW * c:WW * (c + 1)],
+             T.wc[:, WW * c:WW * (c + 1)], T.wp[:, WW * c:WW * (c + 1)], S["e_w%d" % c])
+    both = 2 * engines(partner, core)
+
+    seen = {}
+
+    def tw(name, val):
+        if seen.get(name, 0) < val:
+            te.wait_ge(S[name], val)
+            seen[name] = val
+
+    def stationary(j, t):
+        c = t * HALF // WW
+        if j == pos:
+            tw("k_w%d" % c, 1)
+            return T.wc[:, HALF * t:HALF * (t + 1)], T.wp[:, HALF * t:HALF * (t + 1)]
+        tw("e_w%d" % c, both)
+        return T.pc[:, HALF * t:HALF * (t + 1)], T.pp[:, HALF * t:HALF * (t + 1)]
+
+    def bank(j, i):
+        return T.z[:, (G * j + i) * BANK:(G * j + i) * BANK + HALF]
+
+    def with_x(j, i):
+        a, b = stationary(j, 2 * i + 1)
+        if j == pos:
+            tw("k_xo", n_xo)
+            te.matmul_mx(bank(j, i), a, b, T.xc[:, 0:HALF], T.xp[:, 0:HALF], True, False)
+        else:
+            tw("e_x", both)
+            te.matmul_mx(bank(j, i), a, b, T.ic[:, 0:HALF], T.ip[:, 0:HALF], True, False)
+
+    def with_q(j, i):
+        a, b = stationary(j, 2 * i)
+        if j == 1:
+            tw("k_m", 1)
+            qc, qp = T.qm[:], T.qmp[:]
+        elif k:
+            src = cores[2 * k - 1] if passed[k - 1] and lo[k - 1] == mine else owner(k - 1, mine)
+            tw("arr", 2 * engines(src, core))
+            qc, qp = T.qi[:], T.qip[:]
+        elif head:
+            tw("k_xo", n_xo)
+            qc, qp = T.xc[:, 3 * HALF:4 * HALF], T.xp[:, 3 * HALF:4 * HALF]
+        else:
+            tw("e_x", both)
+            qc, qp = T.ic[:, HALF:2 * HALF], T.ip[:, HALF:2 * HALF]
+        te.matmul_mx(bank(j, i), a, b, qc, qp, False, True).then_inc(S["m%d_%d" % (j, i)], 1)
+
+    if k:
+        for j in (pos, 1 - pos):
+            for i in range(G):
+                with_x(j, i)
+        for i in range(G):
+            with_q(0, i)
+    else:
+        if pos == 1:
+            for i in range(G):
+                with_x(1, i)
+        for i in range(G):
+            with_x(0, i)
+            with_q(0, i)
+        if pos == 0:
+            for i in range(G):
+                with_x(1, i)
+    for i in range(G):
+        with_q(1, i)
+    tw("k_v", 1)
+    if pos == 1:
+        tw("k_o", 1)
+    made = (T.qm, T.qmp) if pos == 0 else (T.qo, T.qop)
+    te.matmul_mx(bank(0, 0), T.vc[:], T.vp[:], made[0][:], made[1][:], True, True).then_inc(S.my0, 1)
+    tw("feed", both)
+    te.matmul_mx(bank(0, 1), T.vc[:], T.vp[:], T.qf[:], T.qfp[:], True, True).then_inc(S.my1, 1)
+
+    for j, h, qc, qp, sem in ((0, T.h0, T.qm, T.qmp, S.k_m), (1, T.h1, T.qo, T.qop, S.k_o)):
+        for i in range(G):
+            if i % 2 == 0:
+                se.wait_ge(S["m%d_%d" % (j, i)], 1)
+                se.activation(h[:, i:EL:G], bank(j, i), ActivationFunctionType.Relu, scale=SCALE).then_inc(S["a%d" % j], 1)
+            else:
+                ve.wait_ge(S["m%d_%d" % (j, i)], 1)
+                ve.tensor_scalar(h[:, i:EL:G], bank(j, i), 0.0, SCALE, AluOpType.max, AluOpType.mult).then_inc(S["a%d" % j], 1)
+        ve.wait_ge(S["a%d" % j], G)
+        ve.quantize_mx(qc[:], qp[:], h[:]).then_inc(sem, 1)
+    if not k:
+        quantise_v()
+
+    jobs = []
+    if pos == 0:
+        if k < last and not passed[k]:
+            jobs.append(("k_o", 1, owner(k + 1, mine), T.qi, T.qip, T.qo, T.qop, S.arr))
+        jobs.append(("k_o", 1, partner, T.qf, T.qfp, T.qo, T.qop, S.feed))
+    else:
+        if k < last:
+            jobs.append(("k_o", 1, owner(k + 1, mine), T.qi, T.qip, T.qo, T.qop, S.arr))
+            if passed[k]:
+                jobs.insert(0 if first[k] else 1, ("feed", both, owner(k + 1, other), T.qi, T.qip, T.qf, T.qfp, S.arr))
+        jobs.append(("k_m", 1, partner, T.qf, T.qfp, T.qm, T.qmp, S.feed))
+    for name, val, dst, dc, dp, sc, sp, sem in jobs:
+        g.wait_ge(S[name], val)
+        send(dst, dc[:], dp[:], sc[:], sp[:], sem)
+    g.wait_ge(S.sent, sent[0])
+
+    ve.wait_ge(S.my0, 1)
+    ve.tensor_copy(T.ys[:, HALF * mine:HALF * (mine + 1)], bank(0, 0)).then_inc(S.cy0, 1)
+    se.wait_ge(S.my1, 1)
+    se.activation(T.ys[:, HALF * other:HALF * (other + 1)], bank(0, 1), ActivationFunctionType.Copy).then_inc(S.cy1, 1)
+    sy.wait_ge(S.cy0, 1)
+    sy.dma_start(T.y[:, HALF * mine:HALF * (mine + 1)], T.ys[:, HALF * mine:HALF * (mine + 1)]).then_inc(S.sy, 16)
+    sy.wait_ge(S.cy1, 1)
+    sy.dma_start(T.y[:, HALF * other:HALF * (other + 1)], T.ys[:, HALF * other:HALF * (other + 1)]).then_inc(S.sy, 16)
+    sy.wait_ge(S.sy, 32)

@@ -1,218 +1,287 @@
 import numpy as np
 from concourse.mybir import dt, AluOpType, ActivationFunctionType
 
+WORLD = 256
 HALF = 128
 EL = 4 * HALF
 G = 4
-WCH = 2
+WCH = 4
 WW = 2 * G * HALF // WCH
+NRL = 4
 SCALE = float(np.float32(0.0301))
 BANK = 512
 
+
+def _pair(name, words):
+    return {name: ("sbuf", [128, words], "float8_e4m3fn_x4"), name + "_p": ("sbuf", [128, words], "uint8")}
+
+
 SCRATCH = {
     "wb": ("sbuf", [128, 2 * G * EL], "bfloat16"),
-    "xb": ("sbuf", [128, 4 * EL], "bfloat16"),
+    "xb": ("sbuf", [128, 2 * EL], "bfloat16"),
+    "sb": ("sbuf", [128, 2 * EL], "bfloat16"),
     "vb": ("sbuf", [128, EL], "bfloat16"),
-    "wc": ("sbuf", [128, 2 * G * HALF], "float8_e4m3fn_x4"), "wp": ("sbuf", [128, 2 * G * HALF], "uint8"),
-    "pc": ("sbuf", [128, 2 * G * HALF], "float8_e4m3fn_x4"), "pp": ("sbuf", [128, 2 * G * HALF], "uint8"),
-    "xc": ("sbuf", [128, 4 * HALF], "float8_e4m3fn_x4"), "xp": ("sbuf", [128, 4 * HALF], "uint8"),
-    "ic": ("sbuf", [128, 2 * HALF], "float8_e4m3fn_x4"), "ip": ("sbuf", [128, 2 * HALF], "uint8"),
-    "vc": ("sbuf", [128, HALF], "float8_e4m3fn_x4"), "vp": ("sbuf", [128, HALF], "uint8"),
-    "qi": ("sbuf", [128, HALF], "float8_e4m3fn_x4"), "qip": ("sbuf", [128, HALF], "uint8"),
-    "qm": ("sbuf", [128, HALF], "float8_e4m3fn_x4"), "qmp": ("sbuf", [128, HALF], "uint8"),
-    "qo": ("sbuf", [128, HALF], "float8_e4m3fn_x4"), "qop": ("sbuf", [128, HALF], "uint8"),
-    "qf": ("sbuf", [128, HALF], "float8_e4m3fn_x4"), "qfp": ("sbuf", [128, HALF], "uint8"),
     "h0": ("sbuf", [128, EL], "bfloat16"), "h1": ("sbuf", [128, EL], "bfloat16"),
     "ys": ("sbuf", [128, 2 * HALF], "float32"),
     "z": ("psum", [128, 2 * G * BANK], "float32"),
 }
-SEMAPHORES = (["l_xp", "l_xo", "l_v", "k_xp", "k_xo", "k_v", "e_x", "arr", "feed", "a0", "a1", "k_m", "k_o",
-               "my0", "my1", "cy0", "cy1", "sy", "sent"]
-              + ["l_w%d" % c for c in range(WCH)] + ["k_w%d" % c for c in range(WCH)] + ["e_w%d" % c for c in range(WCH)]
+for _n, _w in (("wc", 2 * G * HALF),
+               ("pc0", 2 * G * HALF), ("pc1", 2 * G * HALF),
+               ("xc", 2 * HALF), ("sc", 2 * HALF), ("vc", HALF),
+               ("ic0", HALF), ("ic1", HALF),
+               ("qi", HALF), ("qm", HALF), ("qo", HALF),
+               ("qf0", HALF), ("qf1", HALF)):
+    SCRATCH.update(_pair(_n, _w))
+for _i in range(NRL):
+    SCRATCH.update(_pair("rc%d" % _i, HALF))
+
+SEMAPHORES = (["l_v", "k_v", "arr", "feed0", "feed1", "a0", "a1", "k_m", "k_o", "my0", "my1", "cy0", "cy1", "sy", "sent"]
+              + ["%s_%s%d" % (a, b, h) for a in "lk" for b in "xs" for h in range(2)]
+              + ["e_x%d" % j for j in range(2)] + ["rs%d" % i for i in range(NRL)]
+              + ["l_w%d" % c for c in range(WCH)] + ["k_w%d" % c for c in range(WCH)]
+              + ["e_w%d_%d" % (j, c) for j in range(2) for c in range(WCH)]
               + ["m%d_%d" % (j, i) for j in range(2) for i in range(G)])
 
 _CACHE = {}
 
 
+def _pop(mask):
+    return bin(mask).count("1")
+
+
+def _near(topo, a, b):
+    return (topo.host(a), topo.chip(a)) == (topo.host(b), topo.chip(b))
+
+
 def _plan(cores, topo):
-    if "p" in _CACHE:
-        return _CACHE["p"]
-    chips = len(cores) // 2
+    n, chips = len(cores), len(cores) // 2
     for k in range(chips):
-        a, b = cores[2 * k], cores[2 * k + 1]
-        if (topo.host(a), topo.chip(a)) != (topo.host(b), topo.chip(b)):
+        if not _near(topo, cores[2 * k], cores[2 * k + 1]):
             raise ValueError("ranks 2k and 2k+1 must share a chip")
-    hop, step = 3.0, 1.0
+    pairs = list(range(2, chips - 1, 2))
     best = None
-    for code in range(2 ** chips):
-        lo = [(code >> k) & 1 for k in range(chips)]
-        t, done, ok, clash = [0.0, 0.0], [0.0, 0.0], True, 0
-        passed, first = [False] * chips, [False] * chips
-        for k in range(chips):
+    for code in range(2 ** (2 + 3 * len(pairs))):
+        bit = [(code >> b) & 1 for b in range(2 + 3 * len(pairs))]
+        ex = [[None, None] for _ in range(n)]
+        for k, b in ((0, bit[0]), (1, bit[1])):
             for h in (0, 1):
-                done[h] = t[h] + 2 * step if k else (step if lo[0] == h else 2 * step)
-            if k == chips - 1:
-                break
+                ex[2 * k][h] = ex[2 * k + 1][h] = cores[2 * k + (h ^ b)]
+        for m, k in enumerate(pairs):
+            which, order = bit[2 + 3 * m], bit[3 + 3 * m:5 + 3 * m]
             for h in (0, 1):
-                src = cores[2 * k + (0 if lo[k] == h else 1)]
-                dst = cores[2 * k + 2 + (0 if lo[k + 1] == h else 1)]
-                if topo.may_write(src, dst):
-                    t[h] = done[h] + hop
-                elif lo[k] == h and topo.may_write(cores[2 * k + 1], dst):
-                    t[h] = done[h] + 2 * hop
-                    passed[k] = True
-                    first[k] = done[h] + hop < done[1 - h]
-                    clash += abs(done[h] + hop - done[1 - h]) < 2 * step
-                else:
-                    ok = False
-        if not ok:
+                c = k + (h ^ which)
+                ex[2 * k][h] = ex[2 * k + 1][h] = cores[2 * c + order[h]]
+                ex[2 * k + 2][h] = ex[2 * k + 3][h] = cores[2 * c + 1 - order[h]]
+        if not all(ex[r][h] == ex[r + 1][h] or topo.may_write(ex[r][h], ex[r + 1][h]) for r in range(n - 1) for h in (0, 1)):
             continue
-        end = [t[h] + 2 * step + hop if lo[-1] == h else t[h] + step + hop for h in (0, 1)]
-        key = (max(end), clash, sum(end), code)
+        head = 0 if ex[0][0] == cores[0] else 1
+        moves = [(cores[r], ex[r][h]) for r in range(n) for h in (0, 1) if ex[r][h] != cores[r]]
+        key = (ex[n - 1][head] == cores[n - 1],
+               sum(not topo.may_write(a, b) for a, b in moves), sum(not _near(topo, a, b) for a, b in moves), len(moves), code)
         if best is None or key < best[0]:
-            best = (key, lo, passed, first)
-    _CACHE["p"] = best[1:]
-    return _CACHE["p"]
+            best = (key, ex)
+    return best[1]
+
+
+def _units(cores, ex, r):
+    w = [("w", c) for c in range(WCH)]
+    if r < 2:
+        own = 0 if ex[r][0] == cores[r] else 1
+        both = ("x", "s") if r == 0 else ("x",)
+        return [(a, 1 - own) for a in both] + w + [(a, own) for a in both]
+    return w[:WCH // 2] + [("x", 0), ("x", 1)] + w[WCH // 2:]
+
+
+def _build(cores, topo):
+    if "b" in _CACHE:
+        return _CACHE["b"]
+    n = len(cores)
+    ex = _plan(cores, topo)
+    job = {ex[r][h]: (r, h) for r in range(0, n, 2) for h in (0, 1)}
+    sends, relay, expect, slots = {c: [] for c in cores}, {}, {}, {}
+
+    def writers(src, dst):
+        idle = [c for c in range(WORLD) if _near(topo, c, src) and c not in cores]
+        idle.sort(key=lambda c: (-sum(topo.may_write(c, d) for d in cores), c))
+        return ([src] if topo.may_write(src, dst) else []) + [c for c in idle[cores.index(src) % 2::2] if topo.may_write(c, dst)]
+
+    def add(src, wait, sb, lo, hi, dst, db, dlo, sem, near=None, park=None, turn=0):
+        v = src
+        if not _near(topo, src, dst):
+            w = writers(src, dst)
+            v = w[turn % len(w)]
+        if v == src:
+            m = (near if _near(topo, src, dst) else None) or topo.mask(src, dst)
+            sends[src].append((wait, sb, lo, hi, dst, db, dlo, sem, m))
+        else:
+            if park is None:
+                i = slots.get(v, 0)
+                slots[v] = i + 1
+                park = ("rc%d" % i, 0, "rs%d" % i)
+            m1, m = near or topo.mask(src, v), topo.mask(v, dst)
+            sends[src].append((wait, sb, lo, hi, v, park[0], park[1], park[2], m1))
+            relay.setdefault(v, []).append(((park[2], 2 * _pop(m1)), park[0], park[1], park[1] + hi - lo, dst, db, dlo, sem, m))
+        expect[(dst, sem)] = expect.get((dst, sem), 0) + 2 * _pop(m)
+
+    for r, c in enumerate(cores):
+        dests = sorted(set(ex[r]) - {c}, key=lambda d: (_near(topo, c, d), d))
+        far = [d for d in dests if not _near(topo, c, d) and topo.may_write(c, d)]
+        mate = cores[r ^ 1]
+        side = topo.mask(c, mate) & ~topo.mask(c, far[0]) if far else None
+        for a, b in _units(cores, ex, r):
+            if a == "x" and ex[r][b] != c:
+                j = r - job[ex[r][b]][0]
+                add(c, ("k_x%d" % b, 1), "xc", HALF * b, HALF * (b + 1), ex[r][b], "ic%d" % j, 0, "e_x%d" % j)
+            if a == "s" and ex[0][b] != c:
+                add(c, ("k_s%d" % b, 1), "sc", HALF * b, HALF * (b + 1), ex[0][b], "qi", 0, "arr")
+            if a == "w":
+                for d in dests:
+                    j = r - job[d][0]
+                    add(c, ("k_w%d" % b, 1), "wc", WW * b, WW * (b + 1), d, "pc%d" % j, WW * b, "e_w%d_%d" % (j, b),
+                        near=side, park=("pc0", WW * b, "e_w0_%d" % b), turn=b)
+        t0, h = job[c]
+        nxt = ex[t0 + 2][h] if t0 + 2 < n else None
+        if nxt is not None:
+            add(c, ("k_o", 1), "qo", 0, HALF, nxt, "qi", 0, "arr")
+        if cores[t0 + 1] not in (c, nxt):
+            add(c, ("k_o", 1), "qo", 0, HALF, cores[t0 + 1], "qf%d" % h, 0, "feed%d" % h)
+        if cores[t0] != c:
+            add(c, ("k_m", 1), "qm", 0, HALF, cores[t0], "qf%d" % h, 0, "feed%d" % h)
+    _CACHE["b"] = (ex, job, sends, relay, expect)
+    return _CACHE["b"]
 
 
 def rank_program(g, core, T, topo):
+    cores = [int(c) for c in T.cores]
+    ex, job, sends, relay, expect = _build(cores, topo)
+    S = T.sem
+    n = len(cores)
+
+    def run_sends(items):
+        total = 0
+        for wait, sb, lo, hi, dst, db, dlo, sem, mask in items:
+            g.wait_ge(S[wait[0]], wait[1])
+            rid, pid = topo.addr(dst, core)
+            g.remote_dma(T[db][:, dlo:dlo + hi - lo].bitcast(dt.uint8), T[sb][:, lo:hi].bitcast(dt.uint8),
+                         S[sem], S.sent, pid, rid, mask)
+            g.remote_dma(T[db + "_p"][:, dlo:dlo + hi - lo], T[sb + "_p"][:, lo:hi], S[sem], S.sent, pid, rid, mask)
+            total += 2 * _pop(mask)
+        g.wait_ge(S.sent, total)
+
+    if core in relay:
+        run_sends(relay[core])
+        return
     rank = T.rank_of(core)
     if rank is None:
         return
-    cores = [int(c) for c in T.cores]
-    lo, passed, first = _plan(cores, topo)
-    k, pos, last = rank // 2, rank % 2, len(cores) // 2 - 1
-    partner = cores[2 * k + 1 - pos]
-    mine = lo[k] if pos == 0 else 1 - lo[k]
-    other = 1 - mine
-    S, te, ve, se, sy = T.sem, g.tensor, g.vector, g.scalar, g.sync
-    head = rank == 0
-    sent = [0]
+    t0, mine = job[core]
+    te, ve, se, sy = g.tensor, g.vector, g.scalar, g.sync
 
-    def engines(src, dst):
-        return bin(topo.mask(src, dst)).count("1")
-
-    def owner(chip, h):
-        return cores[2 * chip + (0 if lo[chip] == h else 1)]
-
-    def send(dst, dc, dp, sc, sp, sem):
-        rid, pid = topo.addr(dst, core)
-        mask = topo.mask(core, dst)
-        g.remote_dma(dc.bitcast(dt.uint8), sc.bitcast(dt.uint8), sem, S.sent, pid, rid, mask)
-        g.remote_dma(dp, sp, sem, S.sent, pid, rid, mask)
-        sent[0] += 2 * engines(core, dst)
-
-    sy.dma_start(T.xb[:, EL:2 * EL], T.x[:, EL * other:EL * other + EL]).then_inc(S.l_xp, 16)
-    if head:
-        sy.dma_start(T.xb[:, 2 * EL:3 * EL], T.s[:, EL * other:EL * other + EL]).then_inc(S.l_xp, 16)
-    for c in range(WCH):
-        (se if c % 2 == 0 else sy).dma_start(T.wb[:, 4 * WW * c:4 * WW * (c + 1)],
-                                             T.w[:, 4 * WW * c:4 * WW * (c + 1)]).then_inc(S["l_w%d" % c], 16)
-    se.dma_start(T.xb[:, 0:EL], T.x[:, EL * mine:EL * mine + EL]).then_inc(S.l_xo, 16)
-    if head:
-        se.dma_start(T.xb[:, 3 * EL:4 * EL], T.s[:, EL * mine:EL * mine + EL]).then_inc(S.l_xo, 16)
+    for u, (a, b) in enumerate(_units(cores, ex, rank)):
+        q = se if u % 2 == 0 else sy
+        if a == "w":
+            q.dma_start(T.wb[:, 4 * WW * b:4 * WW * (b + 1)], T.w[:, 4 * WW * b:4 * WW * (b + 1)]).then_inc(S["l_w%d" % b], 16)
+            ve.wait_ge(S["l_w%d" % b], 16)
+            ve.quantize_mx(T.wc[:, WW * b:WW * (b + 1)], T.wc_p[:, WW * b:WW * (b + 1)],
+                           T.wb[:, 4 * WW * b:4 * WW * (b + 1)]).then_inc(S["k_w%d" % b], 1)
+        else:
+            raw, inp, cod, pla = (T.xb, T.x, T.xc, T.xc_p) if a == "x" else (T.sb, T.s, T.sc, T.sc_p)
+            q.dma_start(raw[:, EL * b:EL * (b + 1)], inp[:, EL * b:EL * (b + 1)]).then_inc(S["l_%s%d" % (a, b)], 16)
+            ve.wait_ge(S["l_%s%d" % (a, b)], 16)
+            ve.quantize_mx(cod[:, HALF * b:HALF * (b + 1)], pla[:, HALF * b:HALF * (b + 1)],
+                           raw[:, EL * b:EL * (b + 1)]).then_inc(S["k_%s%d" % (a, b)], 1)
     sy.wait_ge(S["k_w%d" % (WCH - 1)], 1)
     sy.dma_start(T.vb[:], T.v[:]).then_inc(S.l_v, 16)
 
-    npar = 2 * HALF if head else HALF
-    ve.wait_ge(S.l_xp, 32 if head else 16)
-    ve.quantize_mx(T.xc[:, HALF:HALF + npar], T.xp[:, HALF:HALF + npar], T.xb[:, EL:EL + 4 * npar]).then_inc(S.k_xp, 1)
-    for c in range(WCH):
-        ve.wait_ge(S["l_w%d" % c], 16)
-        ve.quantize_mx(T.wc[:, WW * c:WW * (c + 1)], T.wp[:, WW * c:WW * (c + 1)],
-                       T.wb[:, 4 * WW * c:4 * WW * (c + 1)]).then_inc(S["k_w%d" % c], 1)
-    ve.wait_ge(S.l_xo, 32 if head else 16)
-    ve.quantize_mx(T.xc[:, 0:HALF], T.xp[:, 0:HALF], T.xb[:, 0:EL]).then_inc(S.k_xo, 1)
-    if head:
-        ve.quantize_mx(T.xc[:, 3 * HALF:4 * HALF], T.xp[:, 3 * HALF:4 * HALF], T.xb[:, 3 * EL:4 * EL]).then_inc(S.k_xo, 1)
-    n_xo = 2 if head else 1
-
     def quantise_v():
         ve.wait_ge(S.l_v, 16)
-        ve.quantize_mx(T.vc[:], T.vp[:], T.vb[:]).then_inc(S.k_v, 1)
+        ve.quantize_mx(T.vc[:], T.vc_p[:], T.vb[:]).then_inc(S.k_v, 1)
 
-    if k:
+    if t0:
         quantise_v()
-
-    g.wait_ge(S.k_xp, 1)
-    send(partner, T.ic[:, 0:npar], T.ip[:, 0:npar], T.xc[:, HALF:HALF + npar], T.xp[:, HALF:HALF + npar], S.e_x)
-    for c in range(WCH):
-        g.wait_ge(S["k_w%d" % c], 1)
-        send(partner, T.pc[:, WW * c:WW * (c + 1)], T.pp[:, WW * c:WW * (c + 1)],
-             T.wc[:, WW * c:WW * (c + 1)], T.wp[:, WW * c:WW * (c + 1)], S["e_w%d" % c])
-    both = 2 * engines(partner, core)
 
     seen = {}
 
-    def tw(name, val):
+    def tw(name, val=None):
+        val = expect[(core, name)] if val is None else val
         if seen.get(name, 0) < val:
             te.wait_ge(S[name], val)
             seen[name] = val
 
+    def cols(name, lo, hi):
+        return T[name][:, lo:hi], T[name + "_p"][:, lo:hi]
+
     def stationary(j, t):
         c = t * HALF // WW
-        if j == pos:
+        if cores[t0 + j] == core:
             tw("k_w%d" % c, 1)
-            return T.wc[:, HALF * t:HALF * (t + 1)], T.wp[:, HALF * t:HALF * (t + 1)]
-        tw("e_w%d" % c, both)
-        return T.pc[:, HALF * t:HALF * (t + 1)], T.pp[:, HALF * t:HALF * (t + 1)]
+            return cols("wc", HALF * t, HALF * (t + 1))
+        tw("e_w%d_%d" % (j, c))
+        return cols("pc%d" % j, HALF * t, HALF * (t + 1))
 
     def bank(j, i):
         return T.z[:, (G * j + i) * BANK:(G * j + i) * BANK + HALF]
 
     def with_x(j, i):
         a, b = stationary(j, 2 * i + 1)
-        if j == pos:
-            tw("k_xo", n_xo)
-            te.matmul_mx(bank(j, i), a, b, T.xc[:, 0:HALF], T.xp[:, 0:HALF], True, False)
+        if cores[t0 + j] == core:
+            tw("k_x%d" % mine, 1)
+            c, d = cols("xc", HALF * mine, HALF * (mine + 1))
         else:
-            tw("e_x", both)
-            te.matmul_mx(bank(j, i), a, b, T.ic[:, 0:HALF], T.ip[:, 0:HALF], True, False)
+            tw("e_x%d" % j)
+            c, d = cols("ic%d" % j, 0, HALF)
+        te.matmul_mx(bank(j, i), a, b, c, d, True, False)
 
     def with_q(j, i):
         a, b = stationary(j, 2 * i)
         if j == 1:
             tw("k_m", 1)
-            qc, qp = T.qm[:], T.qmp[:]
-        elif k:
-            src = cores[2 * k - 1] if passed[k - 1] and lo[k - 1] == mine else owner(k - 1, mine)
-            tw("arr", 2 * engines(src, core))
-            qc, qp = T.qi[:], T.qip[:]
-        elif head:
-            tw("k_xo", n_xo)
-            qc, qp = T.xc[:, 3 * HALF:4 * HALF], T.xp[:, 3 * HALF:4 * HALF]
+            c, d = cols("qm", 0, HALF)
+        elif rank == 0:
+            tw("k_s%d" % mine, 1)
+            c, d = cols("sc", HALF * mine, HALF * (mine + 1))
         else:
-            tw("e_x", both)
-            qc, qp = T.ic[:, HALF:2 * HALF], T.ip[:, HALF:2 * HALF]
-        te.matmul_mx(bank(j, i), a, b, qc, qp, False, True).then_inc(S["m%d_%d" % (j, i)], 1)
+            tw("arr")
+            c, d = cols("qi", 0, HALF)
+        te.matmul_mx(bank(j, i), a, b, c, d, False, True).then_inc(S["m%d_%d" % (j, i)], 1)
 
-    if k:
-        for j in (pos, 1 - pos):
+    if t0:
+        def dist(j):
+            o = cores[t0 + j]
+            return 0 if o == core else 1 if _near(topo, o, core) else 2
+        for j in sorted((0, 1), key=dist):
             for i in range(G):
                 with_x(j, i)
         for i in range(G):
             with_q(0, i)
     else:
-        if pos == 1:
+        if cores[1] == core:
             for i in range(G):
                 with_x(1, i)
         for i in range(G):
             with_x(0, i)
             with_q(0, i)
-        if pos == 0:
+        if cores[1] != core:
             for i in range(G):
                 with_x(1, i)
     for i in range(G):
         with_q(1, i)
+    halves = []
+    for h in (0, 1):
+        if ex[rank][h] == core:
+            halves.append((0, h, "qm", "k_m", 1) if rank == t0 else (0, h, "qo", "k_o", 1))
+        elif rank + 1 < n and ex[rank + 1][h] == core:
+            halves.append((0, h, "qi", "arr", None))
+        else:
+            halves.append((1, h, "qf%d" % h, "feed%d" % h, None))
+    halves.sort()
     tw("k_v", 1)
-    if pos == 1:
-        tw("k_o", 1)
-    made = (T.qm, T.qmp) if pos == 0 else (T.qo, T.qop)
-    te.matmul_mx(bank(0, 0), T.vc[:], T.vp[:], made[0][:], made[1][:], True, True).then_inc(S.my0, 1)
-    tw("feed", both)
-    te.matmul_mx(bank(0, 1), T.vc[:], T.vp[:], T.qf[:], T.qfp[:], True, True).then_inc(S.my1, 1)
+    for u, (_, h, name, sem, val) in enumerate(halves):
+        tw(sem, val)
+        c, d = cols(name, 0, HALF)
+        te.matmul_mx(bank(0, u), T.vc[:], T.vc_p[:], c, d, True, True).then_inc(S["my%d" % u], 1)
 
-    for j, h, qc, qp, sem in ((0, T.h0, T.qm, T.qmp, S.k_m), (1, T.h1, T.qo, T.qop, S.k_o)):
+    for j, h, name, sem in ((0, T.h0, "qm", S.k_m), (1, T.h1, "qo", S.k_o)):
         for i in range(G):
             if i % 2 == 0:
                 se.wait_ge(S["m%d_%d" % (j, i)], 1)
@@ -221,32 +290,19 @@ def rank_program(g, core, T, topo):
                 ve.wait_ge(S["m%d_%d" % (j, i)], 1)
                 ve.tensor_scalar(h[:, i:EL:G], bank(j, i), 0.0, SCALE, AluOpType.max, AluOpType.mult).then_inc(S["a%d" % j], 1)
         ve.wait_ge(S["a%d" % j], G)
-        ve.quantize_mx(qc[:], qp[:], h[:]).then_inc(sem, 1)
-    if not k:
+        ve.quantize_mx(T[name][:], T[name + "_p"][:], h[:]).then_inc(sem, 1)
+    if not t0:
         quantise_v()
 
-    jobs = []
-    if pos == 0:
-        if k < last and not passed[k]:
-            jobs.append(("k_o", 1, owner(k + 1, mine), T.qi, T.qip, T.qo, T.qop, S.arr))
-        jobs.append(("k_o", 1, partner, T.qf, T.qfp, T.qo, T.qop, S.feed))
-    else:
-        if k < last:
-            jobs.append(("k_o", 1, owner(k + 1, mine), T.qi, T.qip, T.qo, T.qop, S.arr))
-            if passed[k]:
-                jobs.insert(0 if first[k] else 1, ("feed", both, owner(k + 1, other), T.qi, T.qip, T.qf, T.qfp, S.arr))
-        jobs.append(("k_m", 1, partner, T.qf, T.qfp, T.qm, T.qmp, S.feed))
-    for name, val, dst, dc, dp, sc, sp, sem in jobs:
-        g.wait_ge(S[name], val)
-        send(dst, dc[:], dp[:], sc[:], sp[:], sem)
-    g.wait_ge(S.sent, sent[0])
+    run_sends(sends[core])
 
+    h0, h1 = halves[0][1], halves[1][1]
     ve.wait_ge(S.my0, 1)
-    ve.tensor_copy(T.ys[:, HALF * mine:HALF * (mine + 1)], bank(0, 0)).then_inc(S.cy0, 1)
+    ve.tensor_copy(T.ys[:, HALF * h0:HALF * (h0 + 1)], bank(0, 0)).then_inc(S.cy0, 1)
     se.wait_ge(S.my1, 1)
-    se.activation(T.ys[:, HALF * other:HALF * (other + 1)], bank(0, 1), ActivationFunctionType.Copy).then_inc(S.cy1, 1)
+    se.activation(T.ys[:, HALF * h1:HALF * (h1 + 1)], bank(0, 1), ActivationFunctionType.Copy).then_inc(S.cy1, 1)
     sy.wait_ge(S.cy0, 1)
-    sy.dma_start(T.y[:, HALF * mine:HALF * (mine + 1)], T.ys[:, HALF * mine:HALF * (mine + 1)]).then_inc(S.sy, 16)
+    sy.dma_start(T.y[:, HALF * h0:HALF * (h0 + 1)], T.ys[:, HALF * h0:HALF * (h0 + 1)]).then_inc(S.sy, 16)
     sy.wait_ge(S.cy1, 1)
-    sy.dma_start(T.y[:, HALF * other:HALF * (other + 1)], T.ys[:, HALF * other:HALF * (other + 1)]).then_inc(S.sy, 16)
+    sy.dma_start(T.y[:, HALF * h1:HALF * (h1 + 1)], T.ys[:, HALF * h1:HALF * (h1 + 1)]).then_inc(S.sy, 16)
     sy.wait_ge(S.sy, 32)

import numpy as np
from concourse.mybir import dt, AluOpType, ActivationFunctionType

WORLD = 256
HALF = 128
EL = 4 * HALF
G = 4
WCH = 4
WW = 2 * G * HALF // WCH
NRL = 4
SCALE = float(np.float32(0.0301))
BANK = 512


def _pair(name, words):
    return {name: ("sbuf", [128, words], "float8_e4m3fn_x4"), name + "_p": ("sbuf", [128, words], "uint8")}


SCRATCH = {
    "wb": ("sbuf", [128, 2 * G * EL], "bfloat16"),
    "xb": ("sbuf", [128, 2 * EL], "bfloat16"),
    "sb": ("sbuf", [128, 2 * EL], "bfloat16"),
    "vb": ("sbuf", [128, EL], "bfloat16"),
    "h0": ("sbuf", [128, EL], "bfloat16"), "h1": ("sbuf", [128, EL], "bfloat16"),
    "ys": ("sbuf", [128, 2 * HALF], "float32"),
    "z": ("psum", [128, 2 * G * BANK], "float32"),
}
for _n, _w in (("wc", 2 * G * HALF),
               ("pc0", 2 * G * HALF), ("pc1", 2 * G * HALF),
               ("xc", 2 * HALF), ("sc", 2 * HALF), ("vc", HALF),
               ("ic0", HALF), ("ic1", HALF),
               ("qi", HALF), ("qm", HALF), ("qo", HALF),
               ("qf0", HALF), ("qf1", HALF)):
    SCRATCH.update(_pair(_n, _w))
for _i in range(NRL):
    SCRATCH.update(_pair("rc%d" % _i, HALF))

SEMAPHORES = (["l_v", "k_v", "arr", "feed0", "feed1", "a0", "a1", "k_m", "k_o", "my0", "my1", "cy0", "cy1", "sy", "sent"]
              + ["%s_%s%d" % (a, b, h) for a in "lk" for b in "xs" for h in range(2)]
              + ["e_x%d" % j for j in range(2)] + ["rs%d" % i for i in range(NRL)]
              + ["l_w%d" % c for c in range(WCH)] + ["k_w%d" % c for c in range(WCH)]
              + ["e_w%d_%d" % (j, c) for j in range(2) for c in range(WCH)]
              + ["m%d_%d" % (j, i) for j in range(2) for i in range(G)])

_CACHE = {}


def _pop(mask):
    return bin(mask).count("1")


def _near(topo, a, b):
    return (topo.host(a), topo.chip(a)) == (topo.host(b), topo.chip(b))


def _plan(cores, topo):
    n, chips = len(cores), len(cores) // 2
    for k in range(chips):
        if not _near(topo, cores[2 * k], cores[2 * k + 1]):
            raise ValueError("ranks 2k and 2k+1 must share a chip")
    pairs = list(range(2, chips - 1, 2))
    best = None
    for code in range(2 ** (2 + 3 * len(pairs))):
        bit = [(code >> b) & 1 for b in range(2 + 3 * len(pairs))]
        ex = [[None, None] for _ in range(n)]
        for k, b in ((0, bit[0]), (1, bit[1])):
            for h in (0, 1):
                ex[2 * k][h] = ex[2 * k + 1][h] = cores[2 * k + (h ^ b)]
        for m, k in enumerate(pairs):
            which, order = bit[2 + 3 * m], bit[3 + 3 * m:5 + 3 * m]
            for h in (0, 1):
                c = k + (h ^ which)
                ex[2 * k][h] = ex[2 * k + 1][h] = cores[2 * c + order[h]]
                ex[2 * k + 2][h] = ex[2 * k + 3][h] = cores[2 * c + 1 - order[h]]
        if not all(ex[r][h] == ex[r + 1][h] or topo.may_write(ex[r][h], ex[r + 1][h]) for r in range(n - 1) for h in (0, 1)):
            continue
        head = 0 if ex[0][0] == cores[0] else 1
        moves = [(cores[r], ex[r][h]) for r in range(n) for h in (0, 1) if ex[r][h] != cores[r]]
        key = (ex[n - 1][head] == cores[n - 1],
               sum(not topo.may_write(a, b) for a, b in moves), sum(not _near(topo, a, b) for a, b in moves), len(moves), code)
        if best is None or key < best[0]:
            best = (key, ex)
    return best[1]


def _units(cores, ex, r):
    w = [("w", c) for c in range(WCH)]
    if r < 2:
        own = 0 if ex[r][0] == cores[r] else 1
        both = ("x", "s") if r == 0 else ("x",)
        return [(a, 1 - own) for a in both] + w + [(a, own) for a in both]
    return w[:WCH // 2] + [("x", 0), ("x", 1)] + w[WCH // 2:]


def _build(cores, topo):
    if "b" in _CACHE:
        return _CACHE["b"]
    n = len(cores)
    ex = _plan(cores, topo)
    job = {ex[r][h]: (r, h) for r in range(0, n, 2) for h in (0, 1)}
    sends, relay, expect, slots = {c: [] for c in cores}, {}, {}, {}

    def writers(src, dst):
        idle = [c for c in range(WORLD) if _near(topo, c, src) and c not in cores]
        idle.sort(key=lambda c: (-sum(topo.may_write(c, d) for d in cores), c))
        return ([src] if topo.may_write(src, dst) else []) + [c for c in idle[cores.index(src) % 2::2] if topo.may_write(c, dst)]

    def add(src, wait, sb, lo, hi, dst, db, dlo, sem, near=None, park=None, turn=0):
        v = src
        if not _near(topo, src, dst):
            w = writers(src, dst)
            v = w[turn % len(w)]
        if v == src:
            m = (near if _near(topo, src, dst) else None) or topo.mask(src, dst)
            sends[src].append((wait, sb, lo, hi, dst, db, dlo, sem, m))
        else:
            if park is None:
                i = slots.get(v, 0)
                slots[v] = i + 1
                park = ("rc%d" % i, 0, "rs%d" % i)
            m1, m = near or topo.mask(src, v), topo.mask(v, dst)
            sends[src].append((wait, sb, lo, hi, v, park[0], park[1], park[2], m1))
            relay.setdefault(v, []).append(((park[2], 2 * _pop(m1)), park[0], park[1], park[1] + hi - lo, dst, db, dlo, sem, m))
        expect[(dst, sem)] = expect.get((dst, sem), 0) + 2 * _pop(m)

    for r, c in enumerate(cores):
        dests = sorted(set(ex[r]) - {c}, key=lambda d: (_near(topo, c, d), d))
        far = [d for d in dests if not _near(topo, c, d) and topo.may_write(c, d)]
        mate = cores[r ^ 1]
        side = topo.mask(c, mate) & ~topo.mask(c, far[0]) if far else None
        for a, b in _units(cores, ex, r):
            if a == "x" and ex[r][b] != c:
                j = r - job[ex[r][b]][0]
                add(c, ("k_x%d" % b, 1), "xc", HALF * b, HALF * (b + 1), ex[r][b], "ic%d" % j, 0, "e_x%d" % j)
            if a == "s" and ex[0][b] != c:
                add(c, ("k_s%d" % b, 1), "sc", HALF * b, HALF * (b + 1), ex[0][b], "qi", 0, "arr")
            if a == "w":
                for d in dests:
                    j = r - job[d][0]
                    add(c, ("k_w%d" % b, 1), "wc", WW * b, WW * (b + 1), d, "pc%d" % j, WW * b, "e_w%d_%d" % (j, b),
                        near=side, park=("pc0", WW * b, "e_w0_%d" % b), turn=b)
        t0, h = job[c]
        nxt = ex[t0 + 2][h] if t0 + 2 < n else None
        if nxt is not None:
            add(c, ("k_o", 1), "qo", 0, HALF, nxt, "qi", 0, "arr")
        if cores[t0 + 1] not in (c, nxt):
            add(c, ("k_o", 1), "qo", 0, HALF, cores[t0 + 1], "qf%d" % h, 0, "feed%d" % h)
        if cores[t0] != c:
            add(c, ("k_m", 1), "qm", 0, HALF, cores[t0], "qf%d" % h, 0, "feed%d" % h)
    _CACHE["b"] = (ex, job, sends, relay, expect)
    return _CACHE["b"]


def rank_program(g, core, T, topo):
    cores = [int(c) for c in T.cores]
    ex, job, sends, relay, expect = _build(cores, topo)
    S = T.sem
    n = len(cores)

    def run_sends(items):
        total = 0
        for wait, sb, lo, hi, dst, db, dlo, sem, mask in items:
            g.wait_ge(S[wait[0]], wait[1])
            rid, pid = topo.addr(dst, core)
            g.remote_dma(T[db][:, dlo:dlo + hi - lo].bitcast(dt.uint8), T[sb][:, lo:hi].bitcast(dt.uint8),
                         S[sem], S.sent, pid, rid, mask)
            g.remote_dma(T[db + "_p"][:, dlo:dlo + hi - lo], T[sb + "_p"][:, lo:hi], S[sem], S.sent, pid, rid, mask)
            total += 2 * _pop(mask)
        g.wait_ge(S.sent, total)

    if core in relay:
        run_sends(relay[core])
        return
    rank = T.rank_of(core)
    if rank is None:
        return
    t0, mine = job[core]
    te, ve, se, sy = g.tensor, g.vector, g.scalar, g.sync

    for u, (a, b) in enumerate(_units(cores, ex, rank)):
        q = se if u % 2 == 0 else sy
        if a == "w":
            q.dma_start(T.wb[:, 4 * WW * b:4 * WW * (b + 1)], T.w[:, 4 * WW * b:4 * WW * (b + 1)]).then_inc(S["l_w%d" % b], 16)
            ve.wait_ge(S["l_w%d" % b], 16)
            ve.quantize_mx(T.wc[:, WW * b:WW * (b + 1)], T.wc_p[:, WW * b:WW * (b + 1)],
                           T.wb[:, 4 * WW * b:4 * WW * (b + 1)]).then_inc(S["k_w%d" % b], 1)
        else:
            raw, inp, cod, pla = (T.xb, T.x, T.xc, T.xc_p) if a == "x" else (T.sb, T.s, T.sc, T.sc_p)
            q.dma_start(raw[:, EL * b:EL * (b + 1)], inp[:, EL * b:EL * (b + 1)]).then_inc(S["l_%s%d" % (a, b)], 16)
            ve.wait_ge(S["l_%s%d" % (a, b)], 16)
            ve.quantize_mx(cod[:, HALF * b:HALF * (b + 1)], pla[:, HALF * b:HALF * (b + 1)],
                           raw[:, EL * b:EL * (b + 1)]).then_inc(S["k_%s%d" % (a, b)], 1)
    sy.wait_ge(S["k_w%d" % (WCH - 1)], 1)
    sy.dma_start(T.vb[:], T.v[:]).then_inc(S.l_v, 16)

    def quantise_v():
        ve.wait_ge(S.l_v, 16)
        ve.quantize_mx(T.vc[:], T.vc_p[:], T.vb[:]).then_inc(S.k_v, 1)

    if t0:
        quantise_v()

    seen = {}

    def tw(name, val=None):
        val = expect[(core, name)] if val is None else val
        if seen.get(name, 0) < val:
            te.wait_ge(S[name], val)
            seen[name] = val

    def cols(name, lo, hi):
        return T[name][:, lo:hi], T[name + "_p"][:, lo:hi]

    def stationary(j, t):
        c = t * HALF // WW
        if cores[t0 + j] == core:
            tw("k_w%d" % c, 1)
            return cols("wc", HALF * t, HALF * (t + 1))
        tw("e_w%d_%d" % (j, c))
        return cols("pc%d" % j, HALF * t, HALF * (t + 1))

    def bank(j, i):
        return T.z[:, (G * j + i) * BANK:(G * j + i) * BANK + HALF]

    def with_x(j, i):
        a, b = stationary(j, 2 * i + 1)
        if cores[t0 + j] == core:
            tw("k_x%d" % mine, 1)
            c, d = cols("xc", HALF * mine, HALF * (mine + 1))
        else:
            tw("e_x%d" % j)
            c, d = cols("ic%d" % j, 0, HALF)
        te.matmul_mx(bank(j, i), a, b, c, d, True, False)

    def with_q(j, i):
        a, b = stationary(j, 2 * i)
        if j == 1:
            tw("k_m", 1)
            c, d = cols("qm", 0, HALF)
        elif rank == 0:
            tw("k_s%d" % mine, 1)
            c, d = cols("sc", HALF * mine, HALF * (mine + 1))
        else:
            tw("arr")
            c, d = cols("qi", 0, HALF)
        te.matmul_mx(bank(j, i), a, b, c, d, False, True).then_inc(S["m%d_%d" % (j, i)], 1)

    if t0:
        def dist(j):
            o = cores[t0 + j]
            return 0 if o == core else 1 if _near(topo, o, core) else 2
        for j in sorted((0, 1), key=dist):
            for i in range(G):
                with_x(j, i)
        for i in range(G):
            with_q(0, i)
    else:
        if cores[1] == core:
            for i in range(G):
                with_x(1, i)
        for i in range(G):
            with_x(0, i)
            with_q(0, i)
        if cores[1] != core:
            for i in range(G):
                with_x(1, i)
    for i in range(G):
        with_q(1, i)
    halves = []
    for h in (0, 1):
        if ex[rank][h] == core:
            halves.append((0, h, "qm", "k_m", 1) if rank == t0 else (0, h, "qo", "k_o", 1))
        elif rank + 1 < n and ex[rank + 1][h] == core:
            halves.append((0, h, "qi", "arr", None))
        else:
            halves.append((1, h, "qf%d" % h, "feed%d" % h, None))
    halves.sort()
    tw("k_v", 1)
    for u, (_, h, name, sem, val) in enumerate(halves):
        tw(sem, val)
        c, d = cols(name, 0, HALF)
        te.matmul_mx(bank(0, u), T.vc[:], T.vc_p[:], c, d, True, True).then_inc(S["my%d" % u], 1)

    for j, h, name, sem in ((0, T.h0, "qm", S.k_m), (1, T.h1, "qo", S.k_o)):
        for i in range(G):
            if i % 2 == 0:
                se.wait_ge(S["m%d_%d" % (j, i)], 1)
                se.activation(h[:, i:EL:G], bank(j, i), ActivationFunctionType.Relu, scale=SCALE).then_inc(S["a%d" % j], 1)
            else:
                ve.wait_ge(S["m%d_%d" % (j, i)], 1)
                ve.tensor_scalar(h[:, i:EL:G], bank(j, i), 0.0, SCALE, AluOpType.max, AluOpType.mult).then_inc(S["a%d" % j], 1)
        ve.wait_ge(S["a%d" % j], G)
        ve.quantize_mx(T[name][:], T[name + "_p"][:], h[:]).then_inc(sem, 1)
    if not t0:
        quantise_v()

    run_sends(sends[core])

    h0, h1 = halves[0][1], halves[1][1]
    ve.wait_ge(S.my0, 1)
    ve.tensor_copy(T.ys[:, HALF * h0:HALF * (h0 + 1)], bank(0, 0)).then_inc(S.cy0, 1)
    se.wait_ge(S.my1, 1)
    se.activation(T.ys[:, HALF * h1:HALF * (h1 + 1)], bank(0, 1), ActivationFunctionType.Copy).then_inc(S.cy1, 1)
    sy.wait_ge(S.cy0, 1)
    sy.dma_start(T.y[:, HALF * h0:HALF * (h0 + 1)], T.ys[:, HALF * h0:HALF * (h0 + 1)]).then_inc(S.sy, 16)
    sy.wait_ge(S.cy1, 1)
    sy.dma_start(T.y[:, HALF * h1:HALF * (h1 + 1)], T.ys[:, HALF * h1:HALF * (h1 + 1)]).then_inc(S.sy, 16)
    sy.wait_ge(S.sy, 32)
